import numpy as np, ml_dtypes
CORES = [12,28,60,100,156,228]
N = 6
import mx_ref
BF = ml_dtypes.bfloat16
def entries(a):
    return np.ascontiguousarray(a.T).reshape(-1)
def table(e):
    return np.ascontiguousarray(np.reshape(e, (-1, 16)).T).astype(np.int32)
def cols(t, e):
    v = np.concatenate([t.reshape(128, -1, 4), np.zeros((128, 1, 4), BF)], axis=1)
    return np.ascontiguousarray(v[:, e]).reshape(128, -1)
def cut(t, i, w=512):
    return t[:, w * i:w * i + w]
def f(rng, *shape):
    return mx_ref.flush((rng.standard_normal(shape, dtype=np.float32) * np.exp2(rng.integers(-2, 3, shape[:-1] + (1,)))).astype(BF))
def wide(rng, *shape, cols=0):
    v = rng.standard_normal(shape, dtype=np.float32) * np.exp2(rng.integers(-12, 13, shape)).astype(np.float32)
    if cols: v *= np.repeat(np.exp2(rng.integers(-cols, cols + 1, shape[:-2] + (1, shape[-1] // 4))) * (rng.random(shape[:-2] + (1, shape[-1] // 4)) > 0.0625), 4, axis=-1).astype(np.float32)
    return mx_ref.flush(v.astype(BF))
T, K, O, CAPP = 256, 4, 2, 48
def lists(rng, foreign=False, own=False, same=False, absent=False):
    S = np.full((N, N, CAPP), -1); M = []
    for s in range(N):
        for d in range(N):
            n = CAPP if foreign else rng.integers(1, CAPP + 1)
            if s != d: S[s, d, rng.permutation(CAPP)[:n]] = rng.integers(0, T, n)
    k = np.arange(K)[:, None]
    for r in range(N):
        far = T + np.flatnonzero(S[:, r].reshape(-1) >= 0)
        m = np.where(rng.random((K, T)) < (1.0 if foreign else np.divide(k + 1, K + 1)), rng.choice(far, (K, T)), rng.integers(0, T, (K, T)))
        there = np.zeros((K, T), bool); there[rng.integers(0, K, T), np.arange(T)] = True
        if absent: there.reshape(-1)[rng.permutation(np.flatnonzero(~there))[:K * T - 2 * K * T // 3 - T]] = True
        else: there |= rng.random((K, T)) >= 0.1 + 0.5 * np.divide(k, K - 1)
        m = np.repeat(m[:, :1], T, axis=1) if same else np.where(there, m, -1)
        if own: m = np.stack([rng.permutation(T) for _ in range(K)])
        M.append(table(m))
    return {"send": np.stack([table(S[s]) for s in range(N)]), "mp": np.stack(M)}
def setup_inputs(rng):
    return {"x": f(rng, N, 128, 4 * T), "w": f(rng, N, 128, K * O * 512), **lists(rng)}
def setup_inputs_absent(rng):
    return {**setup_inputs(rng), **lists(rng, absent=True)}
def setup_inputs_foreign(rng):
    return {**setup_inputs(rng), **lists(rng, foreign=True)}
def setup_inputs_same(rng):
    return {**setup_inputs(rng), **lists(rng, same=True)}
def setup_inputs_spread(rng):
    d = setup_inputs(rng); d["x"] = wide(rng, N, 128, 4 * T); return d
def setup_inputs_own(rng):
    return {**setup_inputs(rng), **lists(rng, own=True)}
def check_inputs(d):
    b = []
    for n in ("x", "w"):
        a = np.abs(d[n].astype(np.float32))
        if not np.isfinite(a).all() or ((a > 0) & ((a < 2.0 ** -30) | (a > 2.0 ** 30))).any(): b.append(n)
    for r in range(N):
        s, m = entries(d["send"][r]), entries(d["mp"][r]).reshape(K, T)
        if s.min() < -1 or s.max() >= T or (s[r * CAPP:(r + 1) * CAPP] != -1).any(): b.append("send")
        held = np.concatenate([entries(d["send"][q])[r * CAPP:(r + 1) * CAPP] for q in range(N)])
        if m.min() < -1 or m.max() >= T + N * CAPP or (held[m[m >= T] - T] < 0).any() or (m < 0).all(axis=0).any(): b.append("mp")
    return b
def reference(x, w, send, mp):
    y = np.zeros((N, 128, O * T), np.float32)
    for r in range(N):
        held = [cols(x[s], entries(send[s])[r * CAPP:(r + 1) * CAPP]) for s in range(N)]
        v = np.concatenate([x[r]] + held, axis=1)
        m = entries(mp[r]).reshape(K, T)
        for k in range(K):
            q = mx_ref.quantize(cols(v, m[k]))
            for o in range(O): y[r][:, T * o:T * o + T] += mx_ref.matmul(mx_ref.quantize(cut(w[r], k * O + o)), q)
    return {"y": y}

from concourse.bass import DstId, RemoteDMATransfer
from concourse.mybir import dt, AluOpType, ActivationFunctionType

COLS, MAPS, O, CAPP, N = 256, 4, 2, 48, 6
UNITS = MAPS * O
SLOTS = (N - 1) * CAPP
WIN = 1 + COLS + SLOTS
LEAST = 128
Copy = ActivationFunctionType.Copy

SCRATCH = {
    "sl": ("sbuf", [128, 18], "int32"),
    "ml": ("sbuf", [128, 64], "int32"),
    "mt": ("sbuf", [128, 64], "int32"),
    "mu": ("sbuf", [128, 64], "int32"),
    "of1": ("sbuf", [128, 16], "uint16"),
    "of2": ("sbuf", [128, 16], "uint16"),
    "ofm": ("sbuf", [128, 64], "uint16"),
    "xb": ("sbuf", [128, 1024], "bfloat16"),
    "wb": ("sbuf", [128, 4096], "bfloat16"),
    "h1": ("sbuf", [128, 768], "bfloat16"),
    "h2": ("sbuf", [128, 576], "bfloat16"),
    "c1": ("sbuf", [128, 192], "float8_e4m3fn_x4"),
    "p1": ("sbuf", [128, 192], "uint8"),
    "c2": ("sbuf", [128, 144], "float8_e4m3fn_x4"),
    "p2": ("sbuf", [128, 144], "uint8"),
    "cv": ("sbuf", [128, COLS + SLOTS], "float8_e4m3fn_x4"),
    "pv": ("sbuf", [128, COLS + SLOTS], "uint8"),
    "cw": ("sbuf", [128, 1024], "float8_e4m3fn_x4"),
    "pw": ("sbuf", [128, 1024], "uint8"),
    "rc": ("sbuf", [128, 2 * CAPP], "float8_e4m3fn_x4"),
    "rp": ("sbuf", [128, 2 * CAPP], "uint8"),
    "y0": ("sbuf", [128, COLS], "float32"),
    "y1": ("sbuf", [128, COLS], "float32"),
}
for _u in range(UNITS):
    SCRATCH["ps%d" % _u] = ("psum", [128, 512], "float32")
    SCRATCH["win%d" % _u] = ("sbuf", [128, 500], "float32")

SEMAPHORES = ["lsend", "lx", "lw0", "lw1", "lmp", "stored", "zero", "pad", "off1", "off2", "g1v", "g1s", "g2v", "g2s",
              "q1", "q2", "qx", "qw0", "qw1", "m1", "m2", "m3", "arr0", "arr1", "left", "rin"]
for _u in range(UNITS):
    SEMAPHORES += [_n + str(_u) for _n in ("om", "oc", "am", "ac", "bm", "bc", "su")]


def bits(engines):
    m = 0
    for e in engines:
        m |= 1 << e
    return m


def runs(ds):
    out = []
    for d in ds:
        if out and out[-1][0] + out[-1][1] == d:
            out[-1][1] += 1
        else:
            out.append([d, 1])
    return out


def split(T, topo, r):
    me = T.cores[r]
    near = [d for d in range(N) if d != r and topo.may_write(me, T.cores[d])]
    far = [d for d in range(N) if d != r and d not in near]
    return near, far


def relays(T, topo, r):
    me = T.cores[r]
    near, far = split(T, topo, r)
    like = [q for q in range(N) if split(T, topo, q)[1] == far or q in near]
    like = sorted(set(like + [r]))
    first = like.index(r) < len(like) // 2
    owners = [c for c in topo.cores_of(me) if c != me and all(topo.may_write(c, T.cores[d]) for d in far)]
    a = [c for c in owners if (topo.die(c) == topo.die(me)) == first]
    b = [c for c in owners if c not in a]
    pairs = [far[i:i + 2] for i in range(0, len(far), 2)]
    if len(pairs) == 1:
        return [(pairs[0], a[0], b[0])]
    return [(pairs[0], a[0], a[1]), (pairs[1], b[0], b[1])]


def near_engines(T, topo, r):
    near, _ = split(T, topo, r)
    e = topo.engines(T.cores[r], T.cores[near[0]])
    h, q = len(e) // 2, len(e) // 4
    if len(near) == 1:
        return [e], [e]
    if len(near) == 3:
        return [e[:h], e[h:h + q], e[h + q:]], [e[h:], e[:q], e[q:h]]
    n = len(e)
    while n * len(near) > len(e):
        n //= 2
    part = [e[i * n:i * n + n] for i in range(len(near))]
    return part, part


def place(r, s):
    return CAPP * (s if s < r else s - 1)


def groups(T, topo, r):
    lead = 0
    for s in range(N):
        if s == r:
            continue
        if r not in split(T, topo, s)[0]:
            break
        lead += CAPP
    return [(0, lead), (lead, SLOTS)] if 2 * CAPP <= lead < SLOTS else [(0, SLOTS)]


def group_of(T, topo, r, s):
    for i, (a, b) in enumerate(groups(T, topo, r)):
        if a <= place(r, s) < b:
            return i


def second_hop(T, topo, relay, pair):
    e = topo.engines(relay, T.cores[pair[0]])
    n = len(e) // len(pair)
    return [e[i * n:i * n + n] for i in range(len(pair))]


def arrivals(T, topo, r):
    total = [0] * len(groups(T, topo, r))
    for s in range(N):
        if s == r:
            continue
        near, far = split(T, topo, s)
        i = group_of(T, topo, r, s)
        if r in near:
            for part in near_engines(T, topo, s):
                total[i] += len(part[near.index(r)])
        else:
            for pair, cc, pc in relays(T, topo, s):
                if r in pair:
                    for c in (cc, pc):
                        total[i] += len(second_hop(T, topo, c, pair)[pair.index(r)])
    return total


def first_hop(T, topo, r):
    me = T.cores[r]
    near, _ = split(T, topo, r)
    rel = relays(T, topo, r)
    low = topo.engines(me, T.cores[near[0]])
    high = [e for e in topo.engines(me, rel[0][1]) if e not in low]
    return [high] if len(rel) == 1 else [high, low]


def send(g, T, topo, core, items, local):
    ts = []
    for d, out, src, eng, sem in items:
        rid, pid = topo.addr(d, core)
        ts.append(RemoteDMATransfer(dst_ids=[DstId(rid=rid, pnc=pid)], dma_engine_mask=bits(eng), remote_sem=sem,
                                    srcs=[src], dsts=[out]))
    if len(items) == 1:
        d, out, src, eng, sem = items[0]
        rid, pid = topo.addr(d, core)
        g.remote_dma(out, src, sem, local, pid, rid, bits(eng))
    else:
        g.remote_dma_fused(ts, local_sem=local)
    return sum(len(i[3]) for i in items)


def slot_codes(T, r, s):
    a = COLS + place(r, s)
    return T.cv[:, a:a + CAPP].bitcast(dt.uint8)


def slot_planes(T, r, s):
    a = COLS + place(r, s)
    return T.pv[:, a:a + CAPP]


def relay_program(g, core, T, topo):
    for r in range(N):
        for i, (pair, cc, pc) in enumerate(relays(T, topo, r)):
            if core not in (cc, pc):
                continue
            S = T.sem
            n = len(first_hop(T, topo, r)[i])
            g.wait_ge(S.rin, n)
            items = []
            for j, (d, eng) in enumerate(zip(pair, second_hop(T, topo, core, pair))):
                a = j * CAPP
                if core == cc:
                    out, src = slot_codes(T, d, r), T.rc[:, a:a + CAPP].bitcast(dt.uint8)
                else:
                    out, src = slot_planes(T, d, r), T.rp[:, a:a + CAPP]
                items.append((T.cores[d], out, src, eng, S["arr%d" % group_of(T, topo, d, r)]))
            g.wait_ge(S.left, send(g, T, topo, core, items, S.left))


def rank_program(g, core, T, topo):
    r = T.rank_of(core)
    if r is None:
        relay_program(g, core, T, topo)
        return
    S = T.sem
    V, A, E, Y = g.vector, g.scalar, g.tensor, g.sync
    near, far = split(T, topo, r)
    rel = relays(T, topo, r)
    n1, n2 = len(far) * CAPP, len(near) * CAPP
    w1, w2 = max(n1, LEAST), max(n2, LEAST)
    grp = groups(T, topo, r)

    for q in range(8):
        (Y if q < 5 else A).dma_start(T.sl[16 * q:16 * q + 16, :], T.send[:, :]).then_inc(S.lsend, 16)
    A.dma_start(T.xb[:, :], T.x[:, :]).then_inc(S.lx, 16)
    Y.dma_start(T.wb[:, 0:2048], T.w[:, 0:2048]).then_inc(S.lw0, 16)
    for q in range(8):
        Y.dma_start(T.ml[16 * q:16 * q + 16, :], T.mp[:, :]).then_inc(S.lmp, 16)
    Y.wait_ge(S.q1, 1)
    Y.dma_start(T.wb[:, 2048:4096], T.w[:, 2048:4096]).then_inc(S.lw1, 16)

    for u in range(UNITS):
        V.memset(T["win%d" % u][:, 0:1], 0.0).then_inc(S.zero, 1)
    pads = 0
    for h, n, w in ((T.h1, n1, w1), (T.h2, n2, w2)):
        if n < w:
            V.memset(h[:, 4 * n:4 * w], 0.0).then_inc(S.pad, 1)
            pads += 1

    def offsets(out, ds, sem):
        at, k = 0, 0
        for d, m in runs(ds):
            V.tensor_scalar(out[:, at:at + 3 * m], T.sl[:, 3 * d:3 * d + 3 * m], 0.0, 4.0, AluOpType.max,
                            AluOpType.mult).then_inc(sem, 1)
            at += 3 * m
            k += 1
        return k

    def picked(t, off, n):
        return T.xb[:, t:4 * COLS].indirect(off[:, 0:n // 16])

    V.wait_ge(S.lsend, 128)
    k1 = offsets(T.of1, far, S.off1)
    V.wait_ge(S.off1, k1)
    V.wait_ge(S.lx, 16)
    for t in (0, 1):
        V.tensor_copy(T.h1[:, t:4 * n1:4], picked(t, T.of1, n1)).then_inc(S.g1v, 1)
    k2 = offsets(T.of2, near, S.off2)
    A.wait_ge(S.off1, k1)
    A.wait_ge(S.lx, 16)
    for t in (2, 3):
        A.activation(T.h1[:, t:4 * n1:4], picked(t, T.of1, n1), Copy).then_inc(S.g1s, 1)
    if pads:
        V.wait_ge(S.pad, pads)
    V.wait_ge(S.g1v, 2)
    V.wait_ge(S.g1s, 2)
    V.quantize_mx(T.c1[:, 0:w1], T.p1[:, 0:w1], T.h1[:, 0:4 * w1]).then_inc(S.q1, 1)
    V.wait_ge(S.off2, k2)
    for t in (0, 1):
        V.tensor_copy(T.h2[:, t:4 * n2:4], picked(t, T.of2, n2)).then_inc(S.g2v, 1)
    A.wait_ge(S.off2, k2)
    for t in (2, 3):
        A.activation(T.h2[:, t:4 * n2:4], picked(t, T.of2, n2), Copy).then_inc(S.g2s, 1)
    V.wait_ge(S.g2v, 2)
    V.wait_ge(S.g2s, 2)
    V.quantize_mx(T.c2[:, 0:w2], T.p2[:, 0:w2], T.h2[:, 0:4 * w2]).then_inc(S.q2, 1)

    sent = 0
    g.wait_ge(S.q1, 1)
    hop = first_hop(T, topo, r)
    for codes in (True, False):
        items = []
        for i, (pair, cc, pc) in enumerate(rel):
            a, m = 2 * CAPP * i, CAPP * len(pair)
            if codes:
                items.append((cc, T.rc[:, 0:m].bitcast(dt.uint8), T.c1[:, a:a + m].bitcast(dt.uint8), hop[i], S.rin))
            else:
                items.append((pc, T.rp[:, 0:m], T.p1[:, a:a + m], hop[i], S.rin))
        sent += send(g, T, topo, core, items, S.left)
    g.wait_ge(S.q2, 1)
    parts = near_engines(T, topo, r)
    for codes in (True, False):
        items = []
        for i, d in enumerate(near):
            a = CAPP * i
            sem = S["arr%d" % group_of(T, topo, d, r)]
            if codes:
                items.append((T.cores[d], slot_codes(T, d, r), T.c2[:, a:a + CAPP].bitcast(dt.uint8), parts[0][i], sem))
            else:
                items.append((T.cores[d], slot_planes(T, d, r), T.p2[:, a:a + CAPP], parts[1][i], sem))
        sent += send(g, T, topo, core, items, S.left)
    g.wait_ge(S.left, sent)

    V.quantize_mx(T.cv[:, 0:COLS], T.pv[:, 0:COLS], T.xb[:, :]).then_inc(S.qx, 1)
    V.wait_ge(S.lw0, 16)
    V.quantize_mx(T.cw[:, 0:512], T.pw[:, 0:512], T.wb[:, 0:2048]).then_inc(S.qw0, 1)
    V.wait_ge(S.lmp, 128)
    V.tensor_scalar(T.mt[:, :], T.ml[:, :], float(COLS + (r + 1) * CAPP), float(-CAPP), AluOpType.is_ge,
                    AluOpType.mult).then_inc(S.m1, 1)
    V.wait_ge(S.m1, 1)
    V.tensor_tensor(T.mu[:, :], T.ml[:, :], T.mt[:, :], AluOpType.add).then_inc(S.m2, 1)
    V.wait_ge(S.lw1, 16)
    V.quantize_mx(T.cw[:, 512:1024], T.pw[:, 512:1024], T.wb[:, 2048:4096]).then_inc(S.qw1, 1)
    V.wait_ge(S.m2, 1)
    V.tensor_scalar(T.ofm[:, :], T.mu[:, :], 1.0, None, AluOpType.add).then_inc(S.m3, 1)

    def product(u, a, b, sem):
        E.matmul_mx(T["ps%d" % u][:, 0:b - a], T.cw[:, 128 * u:128 * u + 128], T.pw[:, 128 * u:128 * u + 128],
                    T.cv[:, a:b], T.pv[:, a:b], True, True).then_inc(sem, 1)

    E.wait_ge(S.qx, 1)
    E.wait_ge(S.qw0, 1)
    for u in range(UNITS):
        if u == UNITS // 2:
            E.wait_ge(S.qw1, 1)
        product(u, 0, COLS, S["om%d" % u])
    total = arrivals(T, topo, r)
    start = []
    last = "oc"
    for i, (a, b) in enumerate(grp):
        start.append(min(COLS + a, COLS + b - LEAST))
        E.wait_ge(S["arr%d" % i], total[i])
        final = i == len(grp) - 1
        for u in range(UNITS):
            E.wait_ge(S[last + str(u)], 1)
            product(u, start[i], COLS + b, S[("bm" if final else "am") + str(u)])
        last = "ac"

    def to_window(q, u, psum_at, at, n, got, done):
        q.wait_ge(S[got + str(u)], 1)
        out, src = T["win%d" % u][:, 1 + at:1 + at + n], T["ps%d" % u][:, psum_at:psum_at + n]
        if q is A:
            q.activation(out, src, Copy).then_inc(S[done + str(u)], 1)
        else:
            q.tensor_copy(out, src).then_inc(S[done + str(u)], 1)

    for u in range(UNITS):
        to_window(A if u < 6 else V, u, 0, 0, COLS, "om", "oc")
    if len(grp) == 2:
        a, b = grp[0]
        for u in range(UNITS):
            to_window(V if u % 2 else A, u, COLS + a - start[0], COLS + a, b - a, "am", "ac")

    a, b = grp[-1]

    def rest(q, u):
        to_window(q, u, COLS + a - start[-1], COLS + a, b - a, "bm", "bc")

    def gathered(u):
        k = u // O
        return T["win%d" % u][:, 0:WIN].indirect(T.ofm[:, 16 * k:16 * k + 16])

    ys = (T.y0, T.y1)
    A.wait_ge(S.zero, UNITS)
    A.wait_ge(S.m3, 1)
    rest(A, 0)
    for u in (0, 1):
        A.wait_ge(S["bc%d" % u], 1)
        A.activation(ys[u][:, :], gathered(u), Copy).then_inc(S["su%d" % u], 1)
    for u in (4, 5, 6, 7):
        rest(A, u)
    V.wait_ge(S.zero, UNITS)
    V.wait_ge(S.m3, 1)
    for u in (1, 2, 3):
        rest(V, u)
    for u in range(O, UNITS):
        V.wait_ge(S["bc%d" % u], 1)
        V.wait_ge(S["su%d" % (u - O)], 1)
        acc = ys[u % O]
        V.tensor_tensor(acc[:, :], gathered(u), acc[:, :], AluOpType.add).then_inc(S["su%d" % u], 1)

    for o in range(O):
        Y.wait_ge(S["su%d" % (UNITS - O + o)], 1)
        Y.dma_start(T.y[:, COLS * o:COLS * o + COLS], ys[o][:, :]).then_inc(S.stored, 16)
    Y.wait_ge(S.stored, 16 * O)
